import numpy as np
CORES = [0,1,2,3,4,5,6,7]
N = 8
def setup_inputs(rng):
    return {"x1": rng.standard_normal((N, 128, 8), dtype=np.float32), "x2": rng.standard_normal((N, 128, 512), dtype=np.float32)}
def reference(x1, x2):
    out = []
    s = x1.sum(axis=0, dtype=np.float64).astype(x1.dtype)
    out.append(np.broadcast_to(s, (N,) + s.shape))
    b = 512 // N
    bl = x2.reshape(N, 128, N, b)
    out.append(np.ascontiguousarray(bl.transpose(2, 1, 0, 3)).reshape(N, 128, 512))
    return {"y1": out[0], "y2": out[1]}

from concourse.bass import DstId, RemoteDMATransfer

N = 8
B = 64

SCRATCH = {
    "gath": ("dram", [N, 128, 8], "float32"),
    "res": ("dram", [128, 8], "float32"),
    "stage": ("sbuf", [128, N * B], "float32"),
    "land": ("sbuf", [128, N * B], "float32"),
}
SEMAPHORES = ["ld1", "ld2", "own2", "arr1", "res1", "arr2", "sent", "stored"]

SUM_MASK = 0xC000


def rank_program(g, core, T, topo):
    r = T.rank_of(core)
    if r is None:
        return
    s = T.sem
    peers = [k for k in range(N) if k != r]

    def dst(k):
        rid, pid, _se = topo.addr(T.cores[k])
        return DstId(rid=rid, pnc=pid)

    g.sync.dma_start(T.gath[r], T.x1[:]).then_inc(s.ld1, 16)
    g.scalar.dma_start(T.stage[:], T.x2[:]).then_inc(s.ld2, 16)
    g.scalar.dma_start(T.land[:, r * B:(r + 1) * B], T.x2[:, r * B:(r + 1) * B]).then_inc(s.own2, 16)

    g.wait_ge(s.ld1, 16)
    g.remote_dma_fused(
        [RemoteDMATransfer(dst_ids=[dst(k) for k in peers], dma_engine_mask=SUM_MASK, remote_sem=s.arr1,
                           srcs=[T.gath[r]], dsts=[T.gath[r] for _k in peers], alu_op=0)],
        local_sem=s.sent)

    g.wait_ge(s.ld2, 16)
    g.remote_dma_fused(
        [RemoteDMATransfer(dst_ids=[dst(j)], dma_engine_mask=0x3 << (2 * i), remote_sem=s.arr2,
                           src=T.stage[:, j * B:(j + 1) * B], dst=T.land[:, r * B:(r + 1) * B], alu_op=0)
         for i, j in enumerate(peers)],
        local_sem=s.sent)

    g.wait_ge(s.arr1, 2 * (N - 1))
    g.remote_dma_fused(
        [RemoteDMATransfer(dst_ids=[dst(r ^ 1)], dma_engine_mask=SUM_MASK, remote_sem=s.res1,
                           srcs=[T.gath[k] for k in range(N)], dsts=[T.res[:]], alu_op=1)],
        local_sem=s.sent)

    g.sync.wait_ge(s.res1, 2)
    g.sync.dma_start(T.y1[:], T.res[:]).then_inc(s.stored, 16)

    g.scalar.wait_ge(s.own2, 16)
    g.scalar.wait_ge(s.arr2, 2 * (N - 1))
    g.scalar.dma_start(T.y2[:], T.land[:]).then_inc(s.stored, 16)

    g.wait_ge(s.sent, 2 + 2 * (N - 1) + 2)
    g.wait_ge(s.stored, 32)
